import numpy as np
CORES = [10,11,138,139,266,267,394,395]
N = 8
GROUPS = [[0,1,2,3],[4,5,6,7]]
def setup_inputs(rng):
    return {"x": rng.standard_normal((N, 128, 4), dtype=np.float32)}
def reference(x):
    y = np.empty((N, 128, 4), x.dtype)
    for g in GROUPS:
        n = len(g); b = x.shape[2] // n
        for i, r in enumerate(g):
            y[r] = np.concatenate([x[s][:, i * b:(i + 1) * b] for s in g], axis=1)
    return {"y": y}

from concourse.bass import DstId, RemoteDMATransfer

SCRATCH = {
    "xs": ("sbuf", [128, 4], "float32"),
    "land": ("sbuf", [128, 4], "float32"),
}
SEMAPHORES = ["loaded", "sent", "filled", "stored"]


def _engine_masks(core, peers, topo):
    out = {}
    for lo, want_same_chip in ((0, False), (8, True)):
        some = [p for p in peers if (topo.mask(core, p) == 0xFFFF) == want_same_chip]
        if not some:
            continue
        share = 8
        while share * len(some) > 8:
            share //= 2
        for k, p in enumerate(some):
            out[p] = (((1 << share) - 1) << (lo + k * share), share)
    return out


def rank_program(g, core, T, topo):
    rank = T.rank_of(core)
    if rank is None:
        return
    group = [grp for grp in T.tables["GROUPS"] if rank in grp][0]
    members = [T.cores[r] for r in group]
    n = len(members)
    i = group.index(rank)
    b = T.x.shape[1] // n

    def blk(t, j):
        return t[:, j * b:(j + 1) * b]

    g.sync.dma_start(T.xs[:], T.x[:]).then_inc(T.sem.loaded, 16)

    peers = [m for m in members if m != core]
    masks = _engine_masks(core, peers, topo)
    transfers = []
    for j, m in enumerate(members):
        if m == core:
            continue
        rid, pid = topo.addr(m, core)
        transfers.append(RemoteDMATransfer(
            dst_ids=[DstId(rid=rid, pnc=pid)], dma_engine_mask=masks[m][0], remote_sem=T.sem.filled,
            src=blk(T.xs, j), dst=blk(T.land, i)))
    g.wait_ge(T.sem.loaded, 16)
    g.remote_dma_fused(transfers, local_sem=T.sem.sent)

    g.scalar.wait_ge(T.sem.loaded, 16)
    g.scalar.dma_start(blk(T.land, i), blk(T.xs, i)).then_inc(T.sem.filled, 16)

    expect = 16
    for m in peers:
        expect += _engine_masks(m, [q for q in members if q != m], topo)[core][1]
    g.sync.wait_ge(T.sem.filled, expect)
    g.sync.dma_start(T.y[:], T.land[:]).then_inc(T.sem.stored, 16)

    g.wait_ge(T.sem.sent, sum(masks[m][1] for m in peers))
    g.wait_ge(T.sem.stored, 16)
